import numpy as np
import ml_dtypes


def mxq(x, axis, fmt="e4m3"):
    dtype, down = {"e4m3": (ml_dtypes.float8_e4m3fn, 7), "e5m2": (ml_dtypes.float8_e5m2, 14)}[fmt]
    v = np.moveaxis(np.asarray(x, np.float32).astype(ml_dtypes.bfloat16).astype(np.float64), axis, -1)
    blocks = v.reshape(v.shape[:-1] + (-1, 32))
    amax = np.abs(blocks).max(-1, keepdims=True)
    byte = np.maximum(np.where(amax > 0, np.frexp(amax)[1] - 1 + 127, 0) - down, 1)
    scale = np.exp2(byte - 127.0)
    codes = (blocks / scale).astype(np.float32).astype(dtype).astype(np.float64)
    return np.moveaxis((codes * scale).reshape(v.shape), -1, axis)


WIDE = False


def mx_kscale(k):
    if not WIDE:
        return np.ones(k)
    levels = np.array([10, -10, 5, -5, 0])
    if k % 512:
        return np.exp2(np.random.permutation(np.resize(levels, k // 32))).repeat(32)
    a = np.empty((k // 512, 16))
    for p in range(k // 512):
        a[p, :8] = np.random.permutation(np.resize(levels, 8))
        for g in range(8):
            far = levels[np.abs(levels - a[p, g]) >= 10]
            a[p, g + 8] = far[np.random.randint(len(far))]
    return np.exp2(a.ravel()).repeat(32)


def f64(x):
    return np.asarray(x).astype(np.float64)


def striped(idx):
    return np.tile(idx.reshape(-1, 16).T, (8, 1)).astype(np.uint16)


def unstriped(offs):
    return offs[:16].T.reshape(-1).astype(np.int64)


E2M1 = np.array([0.0, 0.5, 1.0, 1.5, 2.0, 3.0, 4.0, 6.0, -0.0, -0.5, -1.0, -1.5, -2.0, -3.0, -4.0, -6.0])


def pack_weight(w, fmt):
    k, n = w.shape
    w = f64(np.asarray(w, np.float32).astype(ml_dtypes.bfloat16)).reshape(k // 32, 32, n)
    amax = np.abs(w).max(1)
    if fmt == "e4m3":
        byte = np.frexp(amax)[1] - 1 + 127 - 7
    else:
        mant, ex = np.frexp(amax / 6.0)
        byte = np.where(mant > 0.5, ex, ex - 1) + 127
    byte = np.clip(np.where(amax > 0, byte, 1), 1, 254)
    scaled = (w * np.exp2(127.0 - byte)[:, None, :]).reshape(k, n).astype(np.float32)
    by_word = np.ascontiguousarray(scaled.reshape(k // 512, 128, 4, n).transpose(0, 1, 3, 2))
    if fmt == "e4m3":
        words = by_word.astype(ml_dtypes.float8_e4m3fn).view(np.uint8)
    else:
        c = by_word.astype(ml_dtypes.float4_e2m1fn).view(np.uint8) & 0xF
        words = (c[..., 0::2] | (c[..., 1::2] << 4)).reshape(k // 512, 128, 2 * n)
    return np.ascontiguousarray(words), np.ascontiguousarray(byte.astype(np.uint8).reshape(k // 512, 16, n))


def unpack_weight(words, scales, fmt):
    g, _, n = scales.shape
    words = np.ascontiguousarray(words).reshape(g, 128, n, -1)
    if fmt == "e4m3":
        vals = words.view(ml_dtypes.float8_e4m3fn).astype(np.float64)
    else:
        nib = np.empty((g, 128, n, 4), np.uint8)
        nib[..., 0::2] = words & 0xF
        nib[..., 1::2] = words >> 4
        vals = E2M1[nib]
    vals = vals * np.repeat(np.exp2(scales.astype(np.float64) - 127.0), 8, axis=1)[..., None]
    return vals.transpose(0, 1, 3, 2).reshape(g * 512, n)


def silu(v):
    return v / (1.0 + np.exp(-np.maximum(v, -700.0)))


K, T, E, C, H, TOP, COPIES = 1024, 1024, 4, 128, 512, 2, 768
PAD = 64


def by_expert(wq, xq):
    return np.concatenate([wq[e].T @ xq[:, e * C:(e + 1) * C] for e in range(E)], axis=1)


def setup_inputs():
    n = np.random.standard_normal
    s = mx_kscale(K)
    u = mx_kscale(H)
    left = TOP * T - E * C - COPIES
    deal = np.repeat(np.arange(E + 2), [C] * E + [COPIES, left]).reshape(TOP, T)[:, np.random.permutation(T)]
    deal = np.take_along_axis(deal, np.argsort(np.random.rand(TOP, T), axis=0), axis=0)
    for _ in range(8):
        s_, t_ = np.random.permutation(T).reshape(2, -1); r = np.random.randint(TOP, size=T // 2); x, y = deal[r, s_].copy(), deal[r, t_].copy()
        ok = ~((deal[:, s_] == y).any(0) | (deal[:, t_] == x).any(0)); deal[r[ok], s_[ok]] = y[ok]; deal[r[ok], t_[ok]] = x[ok]
    order = np.lexsort((np.random.rand(TOP * T), deal.reshape(-1)))[:E * C]
    slot_token = order % T
    pos = np.where(deal == E, E * C + np.arange(T), E * C + T + np.arange(T) % PAD).reshape(-1); pos[order] = np.arange(E * C); pos = pos.reshape(TOP, T)
    g = np.random.uniform(0.5, 1.5, (TOP, T)); g = g / g.sum(0)
    xf = n((K, T))
    x = pack_weight(xf * s[:, None], "e4m3")
    w1 = [pack_weight(m, "e4m3") for m in n((E, K, H)) / np.sqrt(K) / s[None, :, None] * u]
    w2 = [pack_weight(m, "e4m3") for m in n((E, H, K)) / np.sqrt(H) / u[None, :, None]]
    return {
        "x_words": x[0],
        "x_scales": x[1],
        "xr": (xf).astype(np.float32),
        "w1_words": np.stack([m[0] for m in w1]),
        "w1_scales": np.stack([m[1] for m in w1]),
        "w2_words": np.stack([m[0] for m in w2]),
        "w2_scales": np.stack([m[1] for m in w2]),
        "gate": np.stack([np.tile(r, (128, 1)) for r in g]).astype(np.float32),
        "offs": striped(slot_token),
        "pos1": striped(pos[0]),
        "pos2": striped(pos[1]),
    }


def reference(x_words, x_scales, xr, w1_words, w1_scales, w2_words, w2_scales, gate, offs, pos1, pos2):
    w1 = np.stack([unpack_weight(w1_words[e], w1_scales[e], "e4m3") for e in range(E)])
    w2 = np.stack([unpack_weight(w2_words[e], w2_scales[e], "e4m3") for e in range(E)])
    idx = unstriped(offs)
    xq = unpack_weight(x_words, x_scales, "e4m3")[:, idx]
    h = silu(by_expert(w1, xq))
    y = by_expert(w2, mxq(h, 0, "e4m3"))
    y = np.concatenate([y, f64(xr), np.zeros((K, PAD))], axis=1)
    out = sum(f64(gate[r, :1]) * y[:, unstriped(p)] for r, p in enumerate((pos1, pos2)))
    return out

@@ -1,0 +1,198 @@
+from contextlib import ExitStack
+
+import concourse.mybir as mybir
+from concourse.masks import make_identity
+
+K, T, E, C, H, PAD = 1024, 1024, 4, 128, 512, 64
+P = 128
+SLOTS = E * C
+WIN = SLOTS + T + PAD
+PASSES = K // 512
+BLOCKS = K // P
+BANK = 512
+
+F32 = mybir.dt.float32
+BF16 = mybir.dt.bfloat16
+I32 = mybir.dt.int32
+U32 = mybir.dt.uint32
+U16 = mybir.dt.uint16
+U8 = mybir.dt.uint8
+FP8X4 = mybir.dt.float8_e4m3fn_x4
+MULT = mybir.AluOpType.mult
+ADD = mybir.AluOpType.add
+SILU = mybir.ActivationFunctionType.Silu
+
+FLOPS = 2 * 2 * SLOTS * K * H
+
+
+def tile_moe_cpy_mlp_silu_kernel(
+    tc, x_words, x_scales, xr, w1_words, w1_scales, w2_words, w2_scales, gate, offs, pos1, pos2, out
+):
+    nc = tc.nc
+    with ExitStack() as ctx:
+        keep = ctx.enter_context(tc.tile_pool(name="keep", bufs=1))
+        ring = ctx.enter_context(tc.tile_pool(name="ring", bufs=3))
+        psum = ctx.enter_context(tc.psum_pool(name="psum", bufs=3))
+        psum_y = ctx.enter_context(tc.psum_pool(name="psum_y", bufs=2))
+
+        offs_sb = keep.tile([P, SLOTS // 16], U16, name="offs_sb")
+        pos_sb = [keep.tile([P, T // 16], U16, name="pos_sb%d" % r) for r in range(2)]
+        xw = [keep.tile([P, T], I32, name="xw%d" % s, align_bytes=64) for s in range(PASSES)]
+        xs = keep.tile([P, T], U8, name="xs", align_bytes=64)
+        w1 = [keep.tile([P, PASSES, H], I32, name="w1_%d" % e, align_bytes=64) for e in range(E)]
+        w1s = keep.tile([P, E * PASSES, H], U8, name="w1s", align_bytes=64)
+        w2 = keep.tile([P, E, K], I32, name="w2", align_bytes=64)
+        w2s = keep.tile([P, K], U8, name="w2s", align_bytes=64)
+        gates = [keep.tile([P, T], F32, name="gates%d" % r) for r in range(2)]
+        window = [keep.tile([P, WIN], F32, name="window%d" % b) for b in range(BLOCKS)]
+        ident = keep.tile([P, P], F32, name="ident")
+        warm = keep.tile([P, 8], F32, name="warm")
+
+        nc.vector.memset(xs[:].bitcast(I32), 0)
+        nc.vector.memset(w1s[:].rearrange("p a i -> p (a i)").bitcast(I32), 0)
+        nc.vector.memset(w2s[:].bitcast(I32), 0)
+        for b in range(BLOCKS):
+            nc.vector.memset(window[b][:, SLOTS + T :], 0.0)
+        nc.scalar.activation(warm[:], window[0][:, SLOTS + T : SLOTS + T + 8], SILU)
+
+        make_identity(nc, ident[:])
+        for q in range(4):
+            nc.gpsimd.dma_start(
+                w2s[32 * q : 32 * q + 4 * E, :].bitcast(I32),
+                w2_scales[:, 0, 4 * q : 4 * q + 4, :].bitcast(I32),
+            )
+        nc.sync.dma_start(xw[0][:], x_words[0].rearrange("p t d -> p (t d)").bitcast(I32))
+        nc.sync.dma_start(offs_sb[:], offs)
+        for q in range(4):
+            nc.sync.dma_start(
+                xs[32 * q : 32 * q + 4 * PASSES, :].bitcast(I32),
+                x_scales[:, 4 * q : 4 * q + 4, :].bitcast(I32),
+            )
+        nc.sync.dma_start(xw[1][:], x_words[1].rearrange("p t d -> p (t d)").bitcast(I32))
+        for q in range(4):
+            nc.sync.dma_start(
+                w1s[32 * q : 32 * q + 4, :, :].bitcast(I32),
+                w1_scales.rearrange("e s b i -> b (e s) i")[4 * q : 4 * q + 4, :, :].bitcast(I32),
+            )
+        for e in range(E):
+            nc.sync.dma_start(w1[e][:], w1_words[e].rearrange("s p i d -> p s (i d)").bitcast(I32))
+        w2_hbm = w2_words.rearrange("e s p n d -> p (e s) (n d)").bitcast(I32)
+
+        def load_w2(first, last):
+            cols = slice(first * P, last * P)
+            nc.sync.dma_start(w2[:, :, cols], w2_hbm[:, :, cols])
+
+        def load_xr(b):
+            nc.sync.dma_start(window[b][:, SLOTS : SLOTS + T], xr[b * P : (b + 1) * P, :])
+
+        load_w2(0, 1)
+        load_xr(0)
+        nc.sync.dma_start(pos_sb[0][:], pos1)
+        nc.sync.dma_start(gates[0][:], gate[0])
+        nc.sync.dma_start(pos_sb[1][:], pos2)
+        nc.sync.dma_start(gates[1][:], gate[1])
+        load_w2(1, 4)
+        load_xr(1)
+        load_xr(2)
+        load_w2(4, 8)
+        for b in range(3, BLOCKS):
+            load_xr(b)
+
+        HALF = SLOTS // 2
+        xg = [[keep.tile([P, HALF], U32, name="xg%d_%d" % (s, h), align_bytes=64) for h in range(2)] for s in range(PASSES)]
+        xsg = [keep.tile([P, HALF], U8, name="xsg%d" % h, align_bytes=64) for h in range(2)]
+        half_offs = [offs_sb[:, h * HALF // 16 : (h + 1) * HALF // 16] for h in range(2)]
+        for h in range(2):
+            nc.vector.tensor_copy(xg[0][h][:], xw[0][:].bitcast(U32).indirect(half_offs[h]))
+        for h in range(2):
+            nc.vector.tensor_copy(xsg[h][:], xs[:].indirect(half_offs[h]))
+            nc.vector.tensor_copy(xg[1][h][:], xw[1][:].bitcast(U32).indirect(half_offs[h]))
+
+        h_codes = [keep.tile([P, C], U32, name="h_codes%d" % e, align_bytes=64) for e in range(E)]
+        h_scales = [keep.tile([P, C], U8, name="h_scales%d" % e, align_bytes=64) for e in range(E)]
+        for e in range(E):
+            cols = slice((e % 2) * C, (e % 2 + 1) * C)
+            pre = psum.tile([P, H], F32, name="pre", tag="turn")
+            for s in range(PASSES):
+                nc.tensor.matmul_mx(
+                    out=pre[:],
+                    lhsT=xg[s][e // 2][:, cols].bitcast(FP8X4),
+                    lhsT_scale=xsg[e // 2][4 * s :, cols],
+                    rhs=w1[e][:, s, :].bitcast(FP8X4),
+                    rhs_scale=w1s[:, e * PASSES + s, :],
+                    start=(s == 0),
+                    stop=(s == PASSES - 1),
+                )
+            act = ring.tile([P, 2, P, 2], BF16, name="act")
+            nc.scalar.activation(act[:], pre[:].rearrange("c (p u j) -> c u p j", u=2, j=2), SILU)
+            pairs = act[:].rearrange("c u p j -> c (u p j)").bitcast(F32)
+            turned = psum.tile([P, 2, C], F32, name="turned", tag="back")
+            for u in range(2):
+                nc.tensor.transpose(turned[:, u, :], pairs[:, u * P : (u + 1) * P], ident[:])
+            grouped = ring.tile([P, 4 * C], BF16, name="grouped", align_bytes=64)
+            nc.scalar.copy(
+                grouped[:].bitcast(F32).rearrange("p (c u) -> p c u", u=2),
+                turned[:].rearrange("p u c -> p c u"),
+            )
+            nc.vector.quantize_mx(out=h_codes[e][:].bitcast(FP8X4), scales=h_scales[e][:], in_=grouped[:])
+
+        def second_layer(b):
+            y = psum_y.tile([P, SLOTS], F32, name="y")
+            rows = slice(b * P, (b + 1) * P)
+            for e in range(E):
+                nc.tensor.matmul_mx(
+                    out=y[:, e * C : (e + 1) * C],
+                    lhsT=w2[:, e, rows].bitcast(FP8X4),
+                    lhsT_scale=w2s[4 * e :, rows],
+                    rhs=h_codes[e][:].bitcast(FP8X4),
+                    rhs_scale=h_scales[e][:],
+                    start=True,
+                    stop=True,
+                )
+            nc.scalar.copy(window[b][:, :SLOTS], y[:])
+
+        def pick(b, r, cols, dst):
+            lists = pos_sb[r][:, cols.start // 16 : cols.stop // 16]
+            nc.vector.tensor_tensor(dst, window[b][:].indirect(lists), gates[r][:, cols], MULT)
+
+        def add_on_tensor(b, terms):
+            total = ring.tile([P, T], F32, name="total")
+            for h in range(T // BANK):
+                summed = psum.tile([P, BANK], F32, name="summed", tag="turn")
+                for j in range(BANK // P):
+                    src = slice(h * BANK + j * P, h * BANK + (j + 1) * P)
+                    for r in range(2):
+                        nc.tensor.matmul(
+                            summed[:, j * P : (j + 1) * P], terms[r][:, src], ident[:],
+                            start=(r == 0), stop=(r == 1), is_transpose=True,
+                        )
+                summed_sb = ring.tile([P, BANK], F32, name="summed_sb")
+                nc.scalar.copy(summed_sb[:], summed[:])
+                back = psum.tile([P, BANK], F32, name="back", tag="back")
+                for j in range(BANK // P):
+                    nc.tensor.transpose(back[:, j * P : (j + 1) * P], summed_sb[:, j * P : (j + 1) * P], ident[:])
+                nc.scalar.copy(total[:, h * BANK : (h + 1) * BANK], back[:])
+            nc.sync.dma_start(out[b * P : (b + 1) * P, :], total[:])
+
+        second_layer(0)
+        for b in range(BLOCKS - 1):
+            terms = [ring.tile([P, T], F32, name="term%d" % r) for r in range(2)]
+            for r in range(2):
+                pick(b, r, slice(0, T), terms[r][:])
+            second_layer(b + 1)
+            add_on_tensor(b, terms)
+
+        b = BLOCKS - 1
+        halves = [slice(0, T // 2), slice(T // 2, T)]
+        last = [[keep.tile([P, T // 2], F32, name="last%d_%d" % (h, r)) for r in range(3)] for h in range(2)]
+
+        def finish(h):
+            nc.vector.tensor_tensor(last[h][2][:], last[h][0][:], last[h][1][:], ADD)
+            nc.sync.dma_start(out[b * P : (b + 1) * P, halves[h]], last[h][2][:])
+
+        pick(b, 0, halves[0], last[0][0][:])
+        pick(b, 1, halves[0], last[0][1][:])
+        pick(b, 0, halves[1], last[1][0][:])
+        finish(0)
+        pick(b, 1, halves[1], last[1][1][:])
+        finish(1)

@@ -10,6 +10,7 @@ WIN = SLOTS + T + PAD
 PASSES = K // 512
 BLOCKS = K // P
 BANK = 512
+ON_TENSOR = 6 * P
 
 F32 = mybir.dt.float32
 BF16 = mybir.dt.bfloat16
@@ -32,14 +33,14 @@ def tile_moe_cpy_mlp_silu_kernel(
     with ExitStack() as ctx:
         keep = ctx.enter_context(tc.tile_pool(name="keep", bufs=1))
         ring = ctx.enter_context(tc.tile_pool(name="ring", bufs=3))
-        psum = ctx.enter_context(tc.psum_pool(name="psum", bufs=3))
-        psum_y = ctx.enter_context(tc.psum_pool(name="psum_y", bufs=2))
+        psum_turn = ctx.enter_context(tc.psum_pool(name="psum_turn", bufs=4))
+        psum = ctx.enter_context(tc.psum_pool(name="psum", bufs=2))
 
         offs_sb = keep.tile([P, SLOTS // 16], U16, name="offs_sb")
         pos_sb = [keep.tile([P, T // 16], U16, name="pos_sb%d" % r) for r in range(2)]
         xw = [keep.tile([P, T], I32, name="xw%d" % s, align_bytes=64) for s in range(PASSES)]
         xs = keep.tile([P, T], U8, name="xs", align_bytes=64)
-        w1 = [keep.tile([P, PASSES, H], I32, name="w1_%d" % e, align_bytes=64) for e in range(E)]
+        w1 = keep.tile([P, PASSES, E, H], I32, name="w1", align_bytes=64)
         w1s = keep.tile([P, E * PASSES, H], U8, name="w1s", align_bytes=64)
         w2 = keep.tile([P, E, K], I32, name="w2", align_bytes=64)
         w2s = keep.tile([P, K], U8, name="w2s", align_bytes=64)
@@ -48,35 +49,22 @@ def tile_moe_cpy_mlp_silu_kernel(
         ident = keep.tile([P, P], F32, name="ident")
         warm = keep.tile([P, 8], F32, name="warm")
 
-        nc.vector.memset(xs[:].bitcast(I32), 0)
+        nc.gpsimd.memset(xs[:].bitcast(I32), 0)
         nc.vector.memset(w1s[:].rearrange("p a i -> p (a i)").bitcast(I32), 0)
         nc.vector.memset(w2s[:].bitcast(I32), 0)
         for b in range(BLOCKS):
             nc.vector.memset(window[b][:, SLOTS + T :], 0.0)
         nc.scalar.activation(warm[:], window[0][:, SLOTS + T : SLOTS + T + 8], SILU)
-
         make_identity(nc, ident[:])
-        for q in range(4):
-            nc.gpsimd.dma_start(
-                w2s[32 * q : 32 * q + 4 * E, :].bitcast(I32),
-                w2_scales[:, 0, 4 * q : 4 * q + 4, :].bitcast(I32),
-            )
-        nc.sync.dma_start(xw[0][:], x_words[0].rearrange("p t d -> p (t d)").bitcast(I32))
-        nc.sync.dma_start(offs_sb[:], offs)
-        for q in range(4):
-            nc.sync.dma_start(
-                xs[32 * q : 32 * q + 4 * PASSES, :].bitcast(I32),
-                x_scales[:, 4 * q : 4 * q + 4, :].bitcast(I32),
-            )
-        nc.sync.dma_start(xw[1][:], x_words[1].rearrange("p t d -> p (t d)").bitcast(I32))
-        for q in range(4):
-            nc.sync.dma_start(
-                w1s[32 * q : 32 * q + 4, :, :].bitcast(I32),
-                w1_scales.rearrange("e s b i -> b (e s) i")[4 * q : 4 * q + 4, :, :].bitcast(I32),
-            )
-        for e in range(E):
-            nc.sync.dma_start(w1[e][:], w1_words[e].rearrange("s p i d -> p s (i d)").bitcast(I32))
+
+        w1_hbm = w1_words.rearrange("e s p i d -> p s e (i d)").bitcast(I32)
         w2_hbm = w2_words.rearrange("e s p n d -> p (e s) (n d)").bitcast(I32)
+
+        def load_x(s):
+            nc.sync.dma_start(xw[s][:], x_words[s].rearrange("p t d -> p (t d)").bitcast(I32))
+
+        def load_w1(s, first, last):
+            nc.sync.dma_start(w1[:, s, first:last, :], w1_hbm[:, s, first:last, :])
 
         def load_w2(first, last):
             cols = slice(first * P, last * P)
@@ -85,12 +73,36 @@ def tile_moe_cpy_mlp_silu_kernel(
         def load_xr(b):
             nc.sync.dma_start(window[b][:, SLOTS : SLOTS + T], xr[b * P : (b + 1) * P, :])
 
+        halves = [slice(0, T // 2), slice(T // 2, T)]
+        load_x(0)
+        for q in range(4):
+            nc.sync.dma_start(
+                xs[32 * q : 32 * q + 4 * PASSES, :].bitcast(I32),
+                x_scales[:, 4 * q : 4 * q + 4, :].bitcast(I32),
+            )
+        nc.sync.dma_start(offs_sb[:], offs)
+        load_w1(0, 0, 2)
+        for q in range(4):
+            nc.sync.dma_start(
+                w1s[32 * q : 32 * q + 4, :, :].bitcast(I32),
+                w1_scales.rearrange("e s b i -> b (e s) i")[4 * q : 4 * q + 4, :, :].bitcast(I32),
+            )
+        load_w1(0, 2, 4)
+        load_x(1)
+        for e in range(E):
+            load_w1(1, e, e + 1)
+        for q in range(4):
+            nc.sync.dma_start(
+                w2s[32 * q : 32 * q + 4 * E, :].bitcast(I32),
+                w2_scales[:, 0, 4 * q : 4 * q + 4, :].bitcast(I32),
+            )
         load_w2(0, 1)
         load_xr(0)
-        nc.sync.dma_start(pos_sb[0][:], pos1)
-        nc.sync.dma_start(gates[0][:], gate[0])
-        nc.sync.dma_start(pos_sb[1][:], pos2)
-        nc.sync.dma_start(gates[1][:], gate[1])
+        for cols in halves:
+            for r, pos in enumerate((pos1, pos2)):
+                if cols.start == 0:
+                    nc.sync.dma_start(pos_sb[r][:], pos)
+                nc.sync.dma_start(gates[r][:, cols], gate[r, :, cols])
         load_w2(1, 4)
         load_xr(1)
         load_xr(2)
@@ -104,41 +116,47 @@ def tile_moe_cpy_mlp_silu_kernel(
         half_offs = [offs_sb[:, h * HALF // 16 : (h + 1) * HALF // 16] for h in range(2)]
         for h in range(2):
             nc.vector.tensor_copy(xg[0][h][:], xw[0][:].bitcast(U32).indirect(half_offs[h]))
-        for h in range(2):
             nc.vector.tensor_copy(xsg[h][:], xs[:].indirect(half_offs[h]))
+        for h in range(2):
             nc.vector.tensor_copy(xg[1][h][:], xw[1][:].bitcast(U32).indirect(half_offs[h]))
 
         h_codes = [keep.tile([P, C], U32, name="h_codes%d" % e, align_bytes=64) for e in range(E)]
         h_scales = [keep.tile([P, C], U8, name="h_scales%d" % e, align_bytes=64) for e in range(E)]
-        for e in range(E):
+        pre = [psum_turn.tile([P, H], F32, name="pre", tag="turn") for e in range(E)]
+
+        def first_layer_pass(e, s):
             cols = slice((e % 2) * C, (e % 2 + 1) * C)
-            pre = psum.tile([P, H], F32, name="pre", tag="turn")
-            for s in range(PASSES):
-                nc.tensor.matmul_mx(
-                    out=pre[:],
-                    lhsT=xg[s][e // 2][:, cols].bitcast(FP8X4),
-                    lhsT_scale=xsg[e // 2][4 * s :, cols],
-                    rhs=w1[e][:, s, :].bitcast(FP8X4),
-                    rhs_scale=w1s[:, e * PASSES + s, :],
-                    start=(s == 0),
-                    stop=(s == PASSES - 1),
-                )
+            nc.tensor.matmul_mx(
+                out=pre[e][:],
+                lhsT=xg[s][e // 2][:, cols].bitcast(FP8X4),
+                lhsT_scale=xsg[e // 2][4 * s :, cols],
+                rhs=w1[:, s, e, :].bitcast(FP8X4),
+                rhs_scale=w1s[:, e * PASSES + s, :],
+                start=(s == 0),
+                stop=(s == PASSES - 1),
+            )
+
+        for e in range(E):
+            first_layer_pass(e, 0)
+        for e in range(E):
+            first_layer_pass(e, 1)
             act = ring.tile([P, 2, P, 2], BF16, name="act")
-            nc.scalar.activation(act[:], pre[:].rearrange("c (p u j) -> c u p j", u=2, j=2), SILU)
+            nc.scalar.activation(act[:], pre[e][:].rearrange("c (p u j) -> c u p j", u=2, j=2), SILU)
             pairs = act[:].rearrange("c u p j -> c (u p j)").bitcast(F32)
             turned = psum.tile([P, 2, C], F32, name="turned", tag="back")
             for u in range(2):
                 nc.tensor.transpose(turned[:, u, :], pairs[:, u * P : (u + 1) * P], ident[:])
             grouped = ring.tile([P, 4 * C], BF16, name="grouped", align_bytes=64)
-            nc.scalar.copy(
+            nc.vector.tensor_copy(
                 grouped[:].bitcast(F32).rearrange("p (c u) -> p c u", u=2),
                 turned[:].rearrange("p u c -> p c u"),
             )
             nc.vector.quantize_mx(out=h_codes[e][:].bitcast(FP8X4), scales=h_scales[e][:], in_=grouped[:])
 
-        def second_layer(b):
-            y = psum_y.tile([P, SLOTS], F32, name="y")
+        def second_layer(b, copy_after):
+            y = psum.tile([P, SLOTS], F32, name="y")
             rows = slice(b * P, (b + 1) * P)
+            done = 0
             for e in range(E):
                 nc.tensor.matmul_mx(
                     out=y[:, e * C : (e + 1) * C],
@@ -149,50 +167,64 @@ def tile_moe_cpy_mlp_silu_kernel(
                     start=True,
                     stop=True,
                 )
-            nc.scalar.copy(window[b][:, :SLOTS], y[:])
+                if e in copy_after:
+                    nc.scalar.copy(window[b][:, done : (e + 1) * C], y[:, done : (e + 1) * C])
+                    done = (e + 1) * C
 
         def pick(b, r, cols, dst):
             lists = pos_sb[r][:, cols.start // 16 : cols.stop // 16]
             nc.vector.tensor_tensor(dst, window[b][:].indirect(lists), gates[r][:, cols], MULT)
 
-        def add_on_tensor(b, terms):
-            total = ring.tile([P, T], F32, name="total")
-            for h in range(T // BANK):
-                summed = psum.tile([P, BANK], F32, name="summed", tag="turn")
-                for j in range(BANK // P):
-                    src = slice(h * BANK + j * P, h * BANK + (j + 1) * P)
+        def add_on_tensor(terms, total):
+            for first in range(0, ON_TENSOR, BANK):
+                width = min(BANK, ON_TENSOR - first)
+                summed = psum_turn.tile([P, width], F32, name="summed", tag="turn")
+                for j in range(0, width, P):
                     for r in range(2):
                         nc.tensor.matmul(
-                            summed[:, j * P : (j + 1) * P], terms[r][:, src], ident[:],
+                            summed[:, j : j + P], terms[r][:, first + j : first + j + P], ident[:],
                             start=(r == 0), stop=(r == 1), is_transpose=True,
                         )
-                summed_sb = ring.tile([P, BANK], F32, name="summed_sb")
+                summed_sb = ring.tile([P, width], F32, name="summed_sb")
                 nc.scalar.copy(summed_sb[:], summed[:])
-                back = psum.tile([P, BANK], F32, name="back", tag="back")
-                for j in range(BANK // P):
-                    nc.tensor.transpose(back[:, j * P : (j + 1) * P], summed_sb[:, j * P : (j + 1) * P], ident[:])
-                nc.scalar.copy(total[:, h * BANK : (h + 1) * BANK], back[:])
+                back = psum.tile([P, width], F32, name="back", tag="back")
+                for j in range(0, width, P):
+                    nc.tensor.transpose(back[:, j : j + P], summed_sb[:, j : j + P], ident[:])
+                nc.scalar.copy(total[:, first : first + width], back[:])
+
+        def finish(b, terms):
+            total = ring.tile([P, T], F32, name="total")
+            nc.vector.tensor_tensor(total[:, ON_TENSOR:], terms[0][:, ON_TENSOR:], terms[1][:, ON_TENSOR:], ADD)
+            add_on_tensor(terms, total)
             nc.sync.dma_start(out[b * P : (b + 1) * P, :], total[:])
 
-        second_layer(0)
-        for b in range(BLOCKS - 1):
-            terms = [ring.tile([P, T], F32, name="term%d" % r) for r in range(2)]
+        second_layer(0, (E - 2, E - 1))
+        second_layer(1, (E - 1,))
+        terms = [ring.tile([P, T], F32, name="term%d" % r) for r in range(2)]
+        for cols in halves:
             for r in range(2):
-                pick(b, r, slice(0, T), terms[r][:])
-            second_layer(b + 1)
-            add_on_tensor(b, terms)
+                pick(0, r, cols, terms[r][:, cols])
+        for b in range(1, BLOCKS - 1):
+            before = terms
+            terms = [ring.tile([P, T], F32, name="term%d" % r) for r in range(2)]
+            pick(b, 0, slice(0, T), terms[0][:])
+            finish(b - 1, before)
+            second_layer(b + 1, (E - 1,))
+            pick(b, 1, slice(0, T), terms[1][:])
 
         b = BLOCKS - 1
-        halves = [slice(0, T // 2), slice(T // 2, T)]
-        last = [[keep.tile([P, T // 2], F32, name="last%d_%d" % (h, r)) for r in range(3)] for h in range(2)]
+        pieces = [slice(0, T // 2), slice(T // 2, 3 * T // 4), slice(3 * T // 4, T)]
+        last = [keep.tile([P, T], F32, name="last%d" % r) for r in range(3)]
 
-        def finish(h):
-            nc.vector.tensor_tensor(last[h][2][:], last[h][0][:], last[h][1][:], ADD)
-            nc.sync.dma_start(out[b * P : (b + 1) * P, halves[h]], last[h][2][:])
+        def finish_piece(cols):
+            nc.vector.tensor_tensor(last[2][:, cols], last[0][:, cols], last[1][:, cols], ADD)
+            nc.sync.dma_start(out[b * P : (b + 1) * P, cols], last[2][:, cols])
 
-        pick(b, 0, halves[0], last[0][0][:])
-        pick(b, 1, halves[0], last[0][1][:])
-        pick(b, 0, halves[1], last[1][0][:])
-        finish(0)
-        pick(b, 1, halves[1], last[1][1][:])
-        finish(1)
+        for i, cols in enumerate(pieces):
+            pick(b, 0, cols, last[0][:, cols])
+            if i == 0:
+                finish(b - 1, terms)
+            else:
+                finish_piece(pieces[i - 1])
+            pick(b, 1, cols, last[1][:, cols])
+        finish_piece(pieces[-1])

@@ -10,7 +10,7 @@ WIN = SLOTS + T + PAD
 PASSES = K // 512
 BLOCKS = K // P
 BANK = 512
-ON_TENSOR = 6 * P
+ON_TENSOR = 7 * P
 
 F32 = mybir.dt.float32
 BF16 = mybir.dt.bfloat16
@@ -32,7 +32,7 @@ def tile_moe_cpy_mlp_silu_kernel(
     nc = tc.nc
     with ExitStack() as ctx:
         keep = ctx.enter_context(tc.tile_pool(name="keep", bufs=1))
-        ring = ctx.enter_context(tc.tile_pool(name="ring", bufs=3))
+        ring = ctx.enter_context(tc.tile_pool(name="ring", bufs=4))
         psum_turn = ctx.enter_context(tc.psum_pool(name="psum_turn", bufs=4))
         psum = ctx.enter_context(tc.psum_pool(name="psum", bufs=2))
 
@@ -40,31 +40,29 @@ def tile_moe_cpy_mlp_silu_kernel(
         pos_sb = [keep.tile([P, T // 16], U16, name="pos_sb%d" % r) for r in range(2)]
         xw = [keep.tile([P, T], I32, name="xw%d" % s, align_bytes=64) for s in range(PASSES)]
         xs = keep.tile([P, T], U8, name="xs", align_bytes=64)
-        w1 = keep.tile([P, PASSES, E, H], I32, name="w1", align_bytes=64)
+        w1 = keep.tile([P, E, PASSES, H], I32, name="w1", align_bytes=64)
         w1s = keep.tile([P, E * PASSES, H], U8, name="w1s", align_bytes=64)
         w2 = keep.tile([P, E, K], I32, name="w2", align_bytes=64)
         w2s = keep.tile([P, K], U8, name="w2s", align_bytes=64)
         gates = [keep.tile([P, T], F32, name="gates%d" % r) for r in range(2)]
         window = [keep.tile([P, WIN], F32, name="window%d" % b) for b in range(BLOCKS)]
         ident = keep.tile([P, P], F32, name="ident")
-        warm = keep.tile([P, 8], F32, name="warm")
 
         nc.gpsimd.memset(xs[:].bitcast(I32), 0)
         nc.vector.memset(w1s[:].rearrange("p a i -> p (a i)").bitcast(I32), 0)
         nc.vector.memset(w2s[:].bitcast(I32), 0)
         for b in range(BLOCKS):
             nc.vector.memset(window[b][:, SLOTS + T :], 0.0)
-        nc.scalar.activation(warm[:], window[0][:, SLOTS + T : SLOTS + T + 8], SILU)
         make_identity(nc, ident[:])
 
-        w1_hbm = w1_words.rearrange("e s p i d -> p s e (i d)").bitcast(I32)
+        w1_hbm = w1_words.rearrange("e s p i d -> p e s (i d)").bitcast(I32)
         w2_hbm = w2_words.rearrange("e s p n d -> p (e s) (n d)").bitcast(I32)
 
         def load_x(s):
             nc.sync.dma_start(xw[s][:], x_words[s].rearrange("p t d -> p (t d)").bitcast(I32))
 
-        def load_w1(s, first, last):
-            nc.sync.dma_start(w1[:, s, first:last, :], w1_hbm[:, s, first:last, :])
+        def load_w1(e, passes, cols):
+            nc.sync.dma_start(w1[:, e, passes, cols], w1_hbm[:, e, passes, cols])
 
         def load_w2(first, last):
             cols = slice(first * P, last * P)
@@ -81,16 +79,20 @@ def tile_moe_cpy_mlp_silu_kernel(
                 x_scales[:, 4 * q : 4 * q + 4, :].bitcast(I32),
             )
         nc.sync.dma_start(offs_sb[:], offs)
-        load_w1(0, 0, 2)
+        parts = [[slice(0, H)]] * (E - 1) + [[slice(0, H // 2), slice(H // 2, H)]]
+        load_w1(0, 0, slice(0, H))
+        load_x(1)
         for q in range(4):
             nc.sync.dma_start(
                 w1s[32 * q : 32 * q + 4, :, :].bitcast(I32),
                 w1_scales.rearrange("e s b i -> b (e s) i")[4 * q : 4 * q + 4, :, :].bitcast(I32),
             )
-        load_w1(0, 2, 4)
-        load_x(1)
-        for e in range(E):
-            load_w1(1, e, e + 1)
+        load_w1(0, 1, slice(0, H))
+        for e in range(1, E - 1):
+            load_w1(e, slice(0, PASSES), slice(0, H))
+        load_w1(E - 1, 0, slice(0, H))
+        for part in parts[E - 1]:
+            load_w1(E - 1, 1, part)
         for q in range(4):
             nc.sync.dma_start(
                 w2s[32 * q : 32 * q + 4 * E, :].bitcast(I32),
@@ -122,54 +124,63 @@ def tile_moe_cpy_mlp_silu_kernel(
 
         h_codes = [keep.tile([P, C], U32, name="h_codes%d" % e, align_bytes=64) for e in range(E)]
         h_scales = [keep.tile([P, C], U8, name="h_scales%d" % e, align_bytes=64) for e in range(E)]
-        pre = [psum_turn.tile([P, H], F32, name="pre", tag="turn") for e in range(E)]
 
-        def first_layer_pass(e, s):
+        def first_layer(e):
             cols = slice((e % 2) * C, (e % 2 + 1) * C)
-            nc.tensor.matmul_mx(
-                out=pre[e][:],
-                lhsT=xg[s][e // 2][:, cols].bitcast(FP8X4),
-                lhsT_scale=xsg[e // 2][4 * s :, cols],
-                rhs=w1[:, s, e, :].bitcast(FP8X4),
-                rhs_scale=w1s[:, e * PASSES + s, :],
-                start=(s == 0),
-                stop=(s == PASSES - 1),
-            )
-
-        for e in range(E):
-            first_layer_pass(e, 0)
-        for e in range(E):
-            first_layer_pass(e, 1)
             act = ring.tile([P, 2, P, 2], BF16, name="act")
-            nc.scalar.activation(act[:], pre[e][:].rearrange("c (p u j) -> c u p j", u=2, j=2), SILU)
+            for part in parts[e]:
+                pre = psum_turn.tile([P, part.stop - part.start], F32, name="pre", tag="turn")
+                for s in range(PASSES):
+                    nc.tensor.matmul_mx(
+                        out=pre[:],
+                        lhsT=xg[s][e // 2][:, cols].bitcast(FP8X4),
+                        lhsT_scale=xsg[e // 2][4 * s :, cols],
+                        rhs=w1[:, e, s, part].bitcast(FP8X4),
+                        rhs_scale=w1s[:, e * PASSES + s, part],
+                        start=(s == 0),
+                        stop=(s == PASSES - 1),
+                    )
+                nc.scalar.activation(
+                    act[:, :, part.start // 4 : part.stop // 4, :],
+                    pre[:].rearrange("c (p u j) -> c u p j", u=2, j=2),
+                    SILU,
+                )
             pairs = act[:].rearrange("c u p j -> c (u p j)").bitcast(F32)
             turned = psum.tile([P, 2, C], F32, name="turned", tag="back")
             for u in range(2):
                 nc.tensor.transpose(turned[:, u, :], pairs[:, u * P : (u + 1) * P], ident[:])
             grouped = ring.tile([P, 4 * C], BF16, name="grouped", align_bytes=64)
-            nc.vector.tensor_copy(
-                grouped[:].bitcast(F32).rearrange("p (c u) -> p c u", u=2),
-                turned[:].rearrange("p u c -> p c u"),
-            )
+            move = nc.scalar.copy if e == E - 1 else nc.vector.tensor_copy
+            move(grouped[:].bitcast(F32).rearrange("p (c u) -> p c u", u=2), turned[:].rearrange("p u c -> p c u"))
             nc.vector.quantize_mx(out=h_codes[e][:].bitcast(FP8X4), scales=h_scales[e][:], in_=grouped[:])
 
-        def second_layer(b, copy_after):
-            y = psum.tile([P, SLOTS], F32, name="y")
+        def expert_rows(y, b, e):
             rows = slice(b * P, (b + 1) * P)
-            done = 0
+            nc.tensor.matmul_mx(
+                out=y[:, e * C : (e + 1) * C],
+                lhsT=w2[:, e, rows].bitcast(FP8X4),
+                lhsT_scale=w2s[4 * e :, rows],
+                rhs=h_codes[e][:].bitcast(FP8X4),
+                rhs_scale=h_scales[e][:],
+                start=True,
+                stop=True,
+            )
+
+        def second_layer(b):
+            y = psum.tile([P, SLOTS], F32, name="y")
             for e in range(E):
-                nc.tensor.matmul_mx(
-                    out=y[:, e * C : (e + 1) * C],
-                    lhsT=w2[:, e, rows].bitcast(FP8X4),
-                    lhsT_scale=w2s[4 * e :, rows],
-                    rhs=h_codes[e][:].bitcast(FP8X4),
-                    rhs_scale=h_scales[e][:],
-                    start=True,
-                    stop=True,
-                )
-                if e in copy_after:
-                    nc.scalar.copy(window[b][:, done : (e + 1) * C], y[:, done : (e + 1) * C])
-                    done = (e + 1) * C
+                expert_rows(y, b, e)
+            nc.scalar.copy(window[b][:, :SLOTS], y[:])
+
+        for e in range(E):
+            first_layer(e)
+        y_early = psum.tile([P, (E - 1) * C], F32, name="y_early", tag="y")
+        for e in range(E - 1):
+            expert_rows(y_early, 0, e)
+        nc.vector.tensor_copy(window[0][:, : (E - 1) * C], y_early[:])
+        y_late = psum.tile([P, SLOTS], F32, name="y_late", tag="y")
+        expert_rows(y_late, 0, E - 1)
+        nc.scalar.copy(window[0][:, (E - 1) * C : SLOTS], y_late[:, (E - 1) * C :])
 
         def pick(b, r, cols, dst):
             lists = pos_sb[r][:, cols.start // 16 : cols.stop // 16]
@@ -196,10 +207,10 @@ def tile_moe_cpy_mlp_silu_kernel(
             total = ring.tile([P, T], F32, name="total")
             nc.vector.tensor_tensor(total[:, ON_TENSOR:], terms[0][:, ON_TENSOR:], terms[1][:, ON_TENSOR:], ADD)
             add_on_tensor(terms, total)
-            nc.sync.dma_start(out[b * P : (b + 1) * P, :], total[:])
+            for cols in halves:
+                nc.sync.dma_start(out[b * P : (b + 1) * P, cols], total[:, cols])
 
-        second_layer(0, (E - 2, E - 1))
-        second_layer(1, (E - 1,))
+        second_layer(1)
         terms = [ring.tile([P, T], F32, name="term%d" % r) for r in range(2)]
         for cols in halves:
             for r in range(2):
@@ -209,11 +220,11 @@ def tile_moe_cpy_mlp_silu_kernel(
             terms = [ring.tile([P, T], F32, name="term%d" % r) for r in range(2)]
             pick(b, 0, slice(0, T), terms[0][:])
             finish(b - 1, before)
-            second_layer(b + 1, (E - 1,))
+            second_layer(b + 1)
             pick(b, 1, slice(0, T), terms[1][:])
 
         b = BLOCKS - 1
-        pieces = [slice(0, T // 2), slice(T // 2, 3 * T // 4), slice(3 * T // 4, T)]
+        pieces = [slice(0, T // 2), slice(T // 2, 7 * T // 8), slice(7 * T // 8, T)]
         last = [keep.tile([P, T], F32, name="last%d" % r) for r in range(3)]
 
         def finish_piece(cols):

@@ -10,7 +10,7 @@ WIN = SLOTS + T + PAD
 PASSES = K // 512
 BLOCKS = K // P
 BANK = 512
-ON_TENSOR = 7 * P
+ON_TENSOR = 5 * P
 
 F32 = mybir.dt.float32
 BF16 = mybir.dt.bfloat16

@@ -10,7 +10,7 @@ WIN = SLOTS + T + PAD
 PASSES = K // 512
 BLOCKS = K // P
 BANK = 512
-ON_TENSOR = 5 * P
+ON_TENSOR = 7 * P
 
 F32 = mybir.dt.float32
 BF16 = mybir.dt.bfloat16
@@ -33,7 +33,6 @@ def tile_moe_cpy_mlp_silu_kernel(
     with ExitStack() as ctx:
         keep = ctx.enter_context(tc.tile_pool(name="keep", bufs=1))
         ring = ctx.enter_context(tc.tile_pool(name="ring", bufs=4))
-        psum_turn = ctx.enter_context(tc.psum_pool(name="psum_turn", bufs=4))
         psum = ctx.enter_context(tc.psum_pool(name="psum", bufs=2))
 
         offs_sb = keep.tile([P, SLOTS // 16], U16, name="offs_sb")
@@ -107,9 +106,8 @@ def tile_moe_cpy_mlp_silu_kernel(
                 nc.sync.dma_start(gates[r][:, cols], gate[r, :, cols])
         load_w2(1, 4)
         load_xr(1)
-        load_xr(2)
         load_w2(4, 8)
-        for b in range(3, BLOCKS):
+        for b in range(2, BLOCKS):
             load_xr(b)
 
         HALF = SLOTS // 2
@@ -129,7 +127,7 @@ def tile_moe_cpy_mlp_silu_kernel(
             cols = slice((e % 2) * C, (e % 2 + 1) * C)
             act = ring.tile([P, 2, P, 2], BF16, name="act")
             for part in parts[e]:
-                pre = psum_turn.tile([P, part.stop - part.start], F32, name="pre", tag="turn")
+                pre = psum.tile([P, part.stop - part.start], F32, name="pre", tag="pre" if part.start == 0 else "summed")
                 for s in range(PASSES):
                     nc.tensor.matmul_mx(
                         out=pre[:],
@@ -189,7 +187,7 @@ def tile_moe_cpy_mlp_silu_kernel(
         def add_on_tensor(terms, total):
             for first in range(0, ON_TENSOR, BANK):
                 width = min(BANK, ON_TENSOR - first)
-                summed = psum_turn.tile([P, width], F32, name="summed", tag="turn")
+                summed = psum.tile([P, width], F32, name="summed", tag="summed")
                 for j in range(0, width, P):
                     for r in range(2):
                         nc.tensor.matmul(
@@ -204,13 +202,14 @@ def tile_moe_cpy_mlp_silu_kernel(
                 nc.scalar.copy(total[:, first : first + width], back[:])
 
         def finish(b, terms):
-            total = ring.tile([P, T], F32, name="total")
+            total = keep.tile([P, T], F32, name="total%d" % b)
             nc.vector.tensor_tensor(total[:, ON_TENSOR:], terms[0][:, ON_TENSOR:], terms[1][:, ON_TENSOR:], ADD)
             add_on_tensor(terms, total)
             for cols in halves:
-                nc.sync.dma_start(out[b * P : (b + 1) * P, cols], total[:, cols])
+                nc.scalar.dma_start(out[b * P : (b + 1) * P, cols], total[:, cols])
 
-        second_layer(1)
+        for b in range(1, BLOCKS):
+            second_layer(b)
         terms = [ring.tile([P, T], F32, name="term%d" % r) for r in range(2)]
         for cols in halves:
             for r in range(2):
@@ -220,7 +219,6 @@ def tile_moe_cpy_mlp_silu_kernel(
             terms = [ring.tile([P, T], F32, name="term%d" % r) for r in range(2)]
             pick(b, 0, slice(0, T), terms[0][:])
             finish(b - 1, before)
-            second_layer(b + 1)
             pick(b, 1, slice(0, T), terms[1][:])
 
         b = BLOCKS - 1

@@ -10,7 +10,6 @@ WIN = SLOTS + T + PAD
 PASSES = K // 512
 BLOCKS = K // P
 BANK = 512
-ON_TENSOR = 7 * P
 
 F32 = mybir.dt.float32
 BF16 = mybir.dt.bfloat16
@@ -40,7 +39,7 @@ def tile_moe_cpy_mlp_silu_kernel(
         xw = [keep.tile([P, T], I32, name="xw%d" % s, align_bytes=64) for s in range(PASSES)]
         xs = keep.tile([P, T], U8, name="xs", align_bytes=64)
         w1 = keep.tile([P, E, PASSES, H], I32, name="w1", align_bytes=64)
-        w1s = keep.tile([P, E * PASSES, H], U8, name="w1s", align_bytes=64)
+        w1s = [keep.tile([P, H], U8, name="w1s%d" % r, align_bytes=64) for r in range(2)]
         w2 = keep.tile([P, E, K], I32, name="w2", align_bytes=64)
         w2s = keep.tile([P, K], U8, name="w2s", align_bytes=64)
         gates = [keep.tile([P, T], F32, name="gates%d" % r) for r in range(2)]
@@ -48,7 +47,8 @@ def tile_moe_cpy_mlp_silu_kernel(
         ident = keep.tile([P, P], F32, name="ident")
 
         nc.gpsimd.memset(xs[:].bitcast(I32), 0)
-        nc.vector.memset(w1s[:].rearrange("p a i -> p (a i)").bitcast(I32), 0)
+        for r in range(2):
+            nc.vector.memset(w1s[r][:].bitcast(I32), 0)
         nc.vector.memset(w2s[:].bitcast(I32), 0)
         for b in range(BLOCKS):
             nc.vector.memset(window[b][:, SLOTS + T :], 0.0)
@@ -71,33 +71,34 @@ def tile_moe_cpy_mlp_silu_kernel(
             nc.sync.dma_start(window[b][:, SLOTS : SLOTS + T], xr[b * P : (b + 1) * P, :])
 
         halves = [slice(0, T // 2), slice(T // 2, T)]
+
+        def load_w1_scales(r):
+            planes = w1_scales.rearrange("e s b i -> (e s) b i")[4 * r : 4 * r + 4]
+            for q in range(4):
+                nc.sync.dma_start(w1s[r][32 * q : 32 * q + 16, :].bitcast(I32), planes[:, 4 * q : 4 * q + 4, :].bitcast(I32))
+
+        parts = [[slice(0, H)]] * E
+        nc.sync.dma_start(offs_sb[:], offs)
         load_x(0)
         for q in range(4):
             nc.sync.dma_start(
                 xs[32 * q : 32 * q + 4 * PASSES, :].bitcast(I32),
                 x_scales[:, 4 * q : 4 * q + 4, :].bitcast(I32),
             )
-        nc.sync.dma_start(offs_sb[:], offs)
-        parts = [[slice(0, H)]] * (E - 1) + [[slice(0, H // 2), slice(H // 2, H)]]
-        load_w1(0, 0, slice(0, H))
         load_x(1)
-        for q in range(4):
-            nc.sync.dma_start(
-                w1s[32 * q : 32 * q + 4, :, :].bitcast(I32),
-                w1_scales.rearrange("e s b i -> b (e s) i")[4 * q : 4 * q + 4, :, :].bitcast(I32),
-            )
-        load_w1(0, 1, slice(0, H))
-        for e in range(1, E - 1):
-            load_w1(e, slice(0, PASSES), slice(0, H))
+        load_w1(0, slice(0, PASSES), slice(0, H))
+        load_w1_scales(0)
+        load_w1(1, slice(0, PASSES), slice(0, H))
+        load_w1(2, slice(0, PASSES), slice(0, H))
+        load_w1_scales(1)
         load_w1(E - 1, 0, slice(0, H))
-        for part in parts[E - 1]:
-            load_w1(E - 1, 1, part)
+        load_w1(E - 1, 1, slice(0, H))
+        load_w2(0, 1)
         for q in range(4):
             nc.sync.dma_start(
                 w2s[32 * q : 32 * q + 4 * E, :].bitcast(I32),
                 w2_scales[:, 0, 4 * q : 4 * q + 4, :].bitcast(I32),
             )
-        load_w2(0, 1)
         load_xr(0)
         for cols in halves:
             for r, pos in enumerate((pos1, pos2)):
@@ -110,31 +111,29 @@ def tile_moe_cpy_mlp_silu_kernel(
         for b in range(2, BLOCKS):
             load_xr(b)
 
-        HALF = SLOTS // 2
-        xg = [[keep.tile([P, HALF], U32, name="xg%d_%d" % (s, h), align_bytes=64) for h in range(2)] for s in range(PASSES)]
-        xsg = [keep.tile([P, HALF], U8, name="xsg%d" % h, align_bytes=64) for h in range(2)]
-        half_offs = [offs_sb[:, h * HALF // 16 : (h + 1) * HALF // 16] for h in range(2)]
-        for h in range(2):
-            nc.vector.tensor_copy(xg[0][h][:], xw[0][:].bitcast(U32).indirect(half_offs[h]))
-            nc.vector.tensor_copy(xsg[h][:], xs[:].indirect(half_offs[h]))
-        for h in range(2):
-            nc.vector.tensor_copy(xg[1][h][:], xw[1][:].bitcast(U32).indirect(half_offs[h]))
+        xsg = keep.tile([P, SLOTS], U8, name="xsg", align_bytes=64)
+        xg = [keep.tile([P, SLOTS], U32, name="xg%d" % s, align_bytes=64) for s in range(PASSES)]
+        for slots in (slice(0, SLOTS // 2), slice(SLOTS // 2, SLOTS)):
+            part_offs = offs_sb[:, slots.start // 16 : slots.stop // 16]
+            nc.vector.tensor_copy(xg[0][:, slots], xw[0][:].bitcast(U32).indirect(part_offs))
+            nc.vector.tensor_copy(xsg[:, slots], xs[:].indirect(part_offs))
+            nc.vector.tensor_copy(xg[1][:, slots], xw[1][:].bitcast(U32).indirect(part_offs))
 
         h_codes = [keep.tile([P, C], U32, name="h_codes%d" % e, align_bytes=64) for e in range(E)]
         h_scales = [keep.tile([P, C], U8, name="h_scales%d" % e, align_bytes=64) for e in range(E)]
 
         def first_layer(e):
-            cols = slice((e % 2) * C, (e % 2 + 1) * C)
+            cols = slice(e * C, (e + 1) * C)
             act = ring.tile([P, 2, P, 2], BF16, name="act")
             for part in parts[e]:
                 pre = psum.tile([P, part.stop - part.start], F32, name="pre", tag="pre" if part.start == 0 else "summed")
                 for s in range(PASSES):
                     nc.tensor.matmul_mx(
                         out=pre[:],
-                        lhsT=xg[s][e // 2][:, cols].bitcast(FP8X4),
-                        lhsT_scale=xsg[e // 2][4 * s :, cols],
+                        lhsT=xg[s][:, cols].bitcast(FP8X4),
+                        lhsT_scale=xsg[4 * s :, cols],
                         rhs=w1[:, e, s, part].bitcast(FP8X4),
-                        rhs_scale=w1s[:, e * PASSES + s, part],
+                        rhs_scale=w1s[e // 2][4 * (PASSES * (e % 2) + s) :, part],
                         start=(s == 0),
                         stop=(s == PASSES - 1),
                     )
@@ -184,28 +183,24 @@ def tile_moe_cpy_mlp_silu_kernel(
             lists = pos_sb[r][:, cols.start // 16 : cols.stop // 16]
             nc.vector.tensor_tensor(dst, window[b][:].indirect(lists), gates[r][:, cols], MULT)
 
-        def add_on_tensor(terms, total):
-            for first in range(0, ON_TENSOR, BANK):
-                width = min(BANK, ON_TENSOR - first)
-                summed = psum.tile([P, width], F32, name="summed", tag="summed")
-                for j in range(0, width, P):
-                    for r in range(2):
-                        nc.tensor.matmul(
-                            summed[:, j : j + P], terms[r][:, first + j : first + j + P], ident[:],
-                            start=(r == 0), stop=(r == 1), is_transpose=True,
-                        )
-                summed_sb = ring.tile([P, width], F32, name="summed_sb")
-                nc.scalar.copy(summed_sb[:], summed[:])
-                back = psum.tile([P, width], F32, name="back", tag="back")
-                for j in range(0, width, P):
-                    nc.tensor.transpose(back[:, j : j + P], summed_sb[:, j : j + P], ident[:])
-                nc.scalar.copy(total[:, first : first + width], back[:])
-
         def finish(b, terms):
             total = keep.tile([P, T], F32, name="total%d" % b)
-            nc.vector.tensor_tensor(total[:, ON_TENSOR:], terms[0][:, ON_TENSOR:], terms[1][:, ON_TENSOR:], ADD)
-            add_on_tensor(terms, total)
+            summed_sb = []
             for cols in halves:
+                summed = psum.tile([P, BANK], F32, name="summed", tag="summed")
+                for j in range(0, BANK, P):
+                    for r in range(2):
+                        nc.tensor.matmul(
+                            summed[:, j : j + P], terms[r][:, cols.start + j : cols.start + j + P], ident[:],
+                            start=(r == 0), stop=(r == 1), is_transpose=True,
+                        )
+                summed_sb.append(ring.tile([P, BANK], F32, name="summed_sb"))
+                nc.scalar.copy(summed_sb[-1][:], summed[:])
+            for cols, turned_sum in zip(halves, summed_sb):
+                back = psum.tile([P, BANK], F32, name="back", tag="back")
+                for j in range(0, BANK, P):
+                    nc.tensor.transpose(back[:, j : j + P], turned_sum[:, j : j + P], ident[:])
+                nc.scalar.copy(total[:, cols], back[:])
                 nc.scalar.dma_start(out[b * P : (b + 1) * P, cols], total[:, cols])
 
         for b in range(1, BLOCKS):

@@ -164,18 +164,18 @@ def tile_moe_cpy_mlp_silu_kernel(
             )
 
         def second_layer(b):
-            y = psum.tile([P, SLOTS], F32, name="y")
+            y = psum.tile([P, SLOTS], F32, name="y", tag="y", bufs=3)
             for e in range(E):
                 expert_rows(y, b, e)
             nc.scalar.copy(window[b][:, :SLOTS], y[:])
 
         for e in range(E):
             first_layer(e)
-        y_early = psum.tile([P, (E - 1) * C], F32, name="y_early", tag="y")
+        y_early = psum.tile([P, (E - 1) * C], F32, name="y_early", tag="y", bufs=3)
         for e in range(E - 1):
             expert_rows(y_early, 0, e)
         nc.vector.tensor_copy(window[0][:, : (E - 1) * C], y_early[:])
-        y_late = psum.tile([P, SLOTS], F32, name="y_late", tag="y")
+        y_late = psum.tile([P, SLOTS], F32, name="y_late", tag="y", bufs=3)
         expert_rows(y_late, 0, E - 1)
         nc.scalar.copy(window[0][:, (E - 1) * C : SLOTS], y_late[:, (E - 1) * C :])
 
@@ -183,11 +183,14 @@ def tile_moe_cpy_mlp_silu_kernel(
             lists = pos_sb[r][:, cols.start // 16 : cols.stop // 16]
             nc.vector.tensor_tensor(dst, window[b][:].indirect(lists), gates[r][:, cols], MULT)
 
+        def new_terms():
+            return [ring.tile([P, T], F32, name="term%d" % r, bufs=3) for r in range(2)]
+
         def finish(b, terms):
             total = keep.tile([P, T], F32, name="total%d" % b)
             summed_sb = []
             for cols in halves:
-                summed = psum.tile([P, BANK], F32, name="summed", tag="summed")
+                summed = psum.tile([P, BANK], F32, name="summed", tag="y", bufs=3)
                 for j in range(0, BANK, P):
                     for r in range(2):
                         nc.tensor.matmul(
@@ -197,7 +200,7 @@ def tile_moe_cpy_mlp_silu_kernel(
                 summed_sb.append(ring.tile([P, BANK], F32, name="summed_sb"))
                 nc.scalar.copy(summed_sb[-1][:], summed[:])
             for cols, turned_sum in zip(halves, summed_sb):
-                back = psum.tile([P, BANK], F32, name="back", tag="back")
+                back = psum.tile([P, BANK], F32, name="back", tag="y", bufs=3)
                 for j in range(0, BANK, P):
                     nc.tensor.transpose(back[:, j : j + P], turned_sum[:, j : j + P], ident[:])
                 nc.scalar.copy(total[:, cols], back[:])
@@ -205,20 +208,20 @@ def tile_moe_cpy_mlp_silu_kernel(
 
         for b in range(1, BLOCKS):
             second_layer(b)
-        terms = [ring.tile([P, T], F32, name="term%d" % r) for r in range(2)]
+        terms = new_terms()
         for cols in halves:
             for r in range(2):
                 pick(0, r, cols, terms[r][:, cols])
         for b in range(1, BLOCKS - 1):
             before = terms
-            terms = [ring.tile([P, T], F32, name="term%d" % r) for r in range(2)]
+            terms = new_terms()
             pick(b, 0, slice(0, T), terms[0][:])
             finish(b - 1, before)
             pick(b, 1, slice(0, T), terms[1][:])
 
         b = BLOCKS - 1
         pieces = [slice(0, T // 2), slice(T // 2, 7 * T // 8), slice(7 * T // 8, T)]
-        last = [keep.tile([P, T], F32, name="last%d" % r) for r in range(3)]
+        last = new_terms() + [keep.tile([P, T], F32, name="last")]
 
         def finish_piece(cols):
             nc.vector.tensor_tensor(last[2][:, cols], last[0][:, cols], last[1][:, cols], ADD)

@@ -10,6 +10,7 @@ WIN = SLOTS + T + PAD
 PASSES = K // 512
 BLOCKS = K // P
 BANK = 512
+RUN = T // P
 
 F32 = mybir.dt.float32
 BF16 = mybir.dt.bfloat16
@@ -43,6 +44,7 @@ def tile_moe_cpy_mlp_silu_kernel(
         w2 = keep.tile([P, E, K], I32, name="w2", align_bytes=64)
         w2s = keep.tile([P, K], U8, name="w2s", align_bytes=64)
         gates = [keep.tile([P, T], F32, name="gates%d" % r) for r in range(2)]
+        gate_row = keep.tile([P, 2, RUN], F32, name="gate_row")
         window = [keep.tile([P, WIN], F32, name="window%d" % b) for b in range(BLOCKS)]
         ident = keep.tile([P, P], F32, name="ident")
 
@@ -79,6 +81,7 @@ def tile_moe_cpy_mlp_silu_kernel(
 
         parts = [[slice(0, H)]] * E
         nc.sync.dma_start(offs_sb[:], offs)
+        nc.sync.dma_start(gate_row[:], gate[:, 0, :].rearrange("r (p m) -> p r m", m=RUN))
         load_x(0)
         for q in range(4):
             nc.sync.dma_start(
@@ -100,16 +103,24 @@ def tile_moe_cpy_mlp_silu_kernel(
                 w2_scales[:, 0, 4 * q : 4 * q + 4, :].bitcast(I32),
             )
         load_xr(0)
-        for cols in halves:
-            for r, pos in enumerate((pos1, pos2)):
-                if cols.start == 0:
-                    nc.sync.dma_start(pos_sb[r][:], pos)
-                nc.sync.dma_start(gates[r][:, cols], gate[r, :, cols])
+        for r, pos in enumerate((pos1, pos2)):
+            nc.sync.dma_start(pos_sb[r][:], pos)
         load_w2(1, 4)
-        load_xr(1)
         load_w2(4, 8)
+        load_xr(1)
         for b in range(2, BLOCKS):
             load_xr(b)
+
+        for r in range(2):
+            for half in range(2):
+                spread = psum.tile([P, RUN // 2, P], F32, name="spread", tag="y", bufs=4)
+                for j in range(RUN // 2):
+                    col = half * RUN // 2 + j
+                    nc.tensor.transpose(spread[:, j, :], gate_row[:, r, col : col + 1].to_broadcast([P, P]), ident[:])
+                nc.scalar.copy(
+                    gates[r][:].rearrange("q (p h j) -> q h p j", h=2, j=RUN // 2)[:, half, :, :],
+                    spread[:].rearrange("q j p -> q p j"),
+                )
 
         xsg = keep.tile([P, SLOTS], U8, name="xsg", align_bytes=64)
         xg = [keep.tile([P, SLOTS], U32, name="xg%d" % s, align_bytes=64) for s in range(PASSES)]
@@ -164,18 +175,18 @@ def tile_moe_cpy_mlp_silu_kernel(
             )
 
         def second_layer(b):
-            y = psum.tile([P, SLOTS], F32, name="y", tag="y", bufs=3)
+            y = psum.tile([P, SLOTS], F32, name="y", tag="y", bufs=4)
             for e in range(E):
                 expert_rows(y, b, e)
             nc.scalar.copy(window[b][:, :SLOTS], y[:])
 
         for e in range(E):
             first_layer(e)
-        y_early = psum.tile([P, (E - 1) * C], F32, name="y_early", tag="y", bufs=3)
+        y_early = psum.tile([P, (E - 1) * C], F32, name="y_early", tag="y", bufs=4)
         for e in range(E - 1):
             expert_rows(y_early, 0, e)
         nc.vector.tensor_copy(window[0][:, : (E - 1) * C], y_early[:])
-        y_late = psum.tile([P, SLOTS], F32, name="y_late", tag="y", bufs=3)
+        y_late = psum.tile([P, SLOTS], F32, name="y_late", tag="y", bufs=4)
         expert_rows(y_late, 0, E - 1)
         nc.scalar.copy(window[0][:, (E - 1) * C : SLOTS], y_late[:, (E - 1) * C :])
 
@@ -183,35 +194,36 @@ def tile_moe_cpy_mlp_silu_kernel(
             lists = pos_sb[r][:, cols.start // 16 : cols.stop // 16]
             nc.vector.tensor_tensor(dst, window[b][:].indirect(lists), gates[r][:, cols], MULT)
 
+        thirds = [slice(0, 3 * P), slice(3 * P, 6 * P), slice(6 * P, T)]
+
         def new_terms():
             return [ring.tile([P, T], F32, name="term%d" % r, bufs=3) for r in range(2)]
 
         def finish(b, terms):
             total = keep.tile([P, T], F32, name="total%d" % b)
-            summed_sb = []
-            for cols in halves:
-                summed = psum.tile([P, BANK], F32, name="summed", tag="y", bufs=3)
-                for j in range(0, BANK, P):
+            turned_sum = ring.tile([P, T], F32, name="turned_sum", bufs=2)
+            for cols in thirds:
+                summed = psum.tile([P, cols.stop - cols.start], F32, name="summed", tag="y", bufs=4)
+                for j in range(cols.start, cols.stop, P):
                     for r in range(2):
                         nc.tensor.matmul(
-                            summed[:, j : j + P], terms[r][:, cols.start + j : cols.start + j + P], ident[:],
+                            summed[:, j - cols.start : j - cols.start + P], terms[r][:, j : j + P], ident[:],
                             start=(r == 0), stop=(r == 1), is_transpose=True,
                         )
-                summed_sb.append(ring.tile([P, BANK], F32, name="summed_sb"))
-                nc.scalar.copy(summed_sb[-1][:], summed[:])
-            for cols, turned_sum in zip(halves, summed_sb):
-                back = psum.tile([P, BANK], F32, name="back", tag="y", bufs=3)
+                nc.scalar.copy(turned_sum[:, cols], summed[:])
+            queue = nc.scalar if b >= BLOCKS - 3 else nc.sync
+            for cols in halves:
+                back = psum.tile([P, BANK], F32, name="back", tag="y", bufs=4)
                 for j in range(0, BANK, P):
-                    nc.tensor.transpose(back[:, j : j + P], turned_sum[:, j : j + P], ident[:])
+                    nc.tensor.transpose(back[:, j : j + P], turned_sum[:, cols.start + j : cols.start + j + P], ident[:])
                 nc.scalar.copy(total[:, cols], back[:])
-                nc.scalar.dma_start(out[b * P : (b + 1) * P, cols], total[:, cols])
+                queue.dma_start(out[b * P : (b + 1) * P, cols], total[:, cols])
 
         for b in range(1, BLOCKS):
             second_layer(b)
         terms = new_terms()
-        for cols in halves:
-            for r in range(2):
-                pick(0, r, cols, terms[r][:, cols])
+        for r in range(2):
+            pick(0, r, slice(0, T), terms[r][:])
         for b in range(1, BLOCKS - 1):
             before = terms
             terms = new_terms()
@@ -221,7 +233,7 @@ def tile_moe_cpy_mlp_silu_kernel(
 
         b = BLOCKS - 1
         pieces = [slice(0, T // 2), slice(T // 2, 7 * T // 8), slice(7 * T // 8, T)]
-        last = new_terms() + [keep.tile([P, T], F32, name="last")]
+        last = new_terms()
 
         def finish_piece(cols):
             nc.vector.tensor_tensor(last[2][:, cols], last[0][:, cols], last[1][:, cols], ADD)
@@ -231,6 +243,7 @@ def tile_moe_cpy_mlp_silu_kernel(
             pick(b, 0, cols, last[0][:, cols])
             if i == 0:
                 finish(b - 1, terms)
+                last.append(ring.tile([P, T], F32, name="last", tag="turned_sum", bufs=2))
             else:
                 finish_piece(pieces[i - 1])
             pick(b, 1, cols, last[1][:, cols])

@@ -11,6 +11,7 @@ PASSES = K // 512
 BLOCKS = K // P
 BANK = 512
 RUN = T // P
+ON_VECTOR = 2
 
 F32 = mybir.dt.float32
 BF16 = mybir.dt.bfloat16
@@ -194,15 +195,22 @@ def tile_moe_cpy_mlp_silu_kernel(
             lists = pos_sb[r][:, cols.start // 16 : cols.stop // 16]
             nc.vector.tensor_tensor(dst, window[b][:].indirect(lists), gates[r][:, cols], MULT)
 
-        thirds = [slice(0, 3 * P), slice(3 * P, 6 * P), slice(6 * P, T)]
-
         def new_terms():
             return [ring.tile([P, T], F32, name="term%d" % r, bufs=3) for r in range(2)]
 
         def finish(b, terms):
+            rows = slice(b * P, (b + 1) * P)
             total = keep.tile([P, T], F32, name="total%d" % b)
+            queue = nc.scalar if b >= BLOCKS - 3 else nc.sync
+            squares = T // P
+            if b == BLOCKS - 2:
+                squares -= ON_VECTOR
+                cols = slice(squares * P, T)
+                nc.vector.tensor_tensor(total[:, cols], terms[0][:, cols], terms[1][:, cols], ADD)
+            third = -(-squares // 3) * P
             turned_sum = ring.tile([P, T], F32, name="turned_sum", bufs=2)
-            for cols in thirds:
+            for first in range(0, squares * P, third):
+                cols = slice(first, min(first + third, squares * P))
                 summed = psum.tile([P, cols.stop - cols.start], F32, name="summed", tag="y", bufs=4)
                 for j in range(cols.start, cols.stop, P):
                     for r in range(2):
@@ -211,13 +219,13 @@ def tile_moe_cpy_mlp_silu_kernel(
                             start=(r == 0), stop=(r == 1), is_transpose=True,
                         )
                 nc.scalar.copy(turned_sum[:, cols], summed[:])
-            queue = nc.scalar if b >= BLOCKS - 3 else nc.sync
-            for cols in halves:
-                back = psum.tile([P, BANK], F32, name="back", tag="y", bufs=4)
-                for j in range(0, BANK, P):
-                    nc.tensor.transpose(back[:, j : j + P], turned_sum[:, cols.start + j : cols.start + j + P], ident[:])
+            for first in range(0, squares * P, BANK):
+                cols = slice(first, min(first + BANK, squares * P))
+                back = psum.tile([P, cols.stop - cols.start], F32, name="back", tag="y", bufs=4)
+                for j in range(cols.start, cols.stop, P):
+                    nc.tensor.transpose(back[:, j - cols.start : j - cols.start + P], turned_sum[:, j : j + P], ident[:])
                 nc.scalar.copy(total[:, cols], back[:])
-                queue.dma_start(out[b * P : (b + 1) * P, cols], total[:, cols])
+                queue.dma_start(out[rows, first : first + BANK], total[:, first : first + BANK])
 
         for b in range(1, BLOCKS):
             second_layer(b)

@@ -11,7 +11,7 @@ PASSES = K // 512
 BLOCKS = K // P
 BANK = 512
 RUN = T // P
-ON_VECTOR = 2
+RELIEVED = range(2, BLOCKS - 1)
 
 F32 = mybir.dt.float32
 BF16 = mybir.dt.bfloat16
@@ -200,11 +200,11 @@ def tile_moe_cpy_mlp_silu_kernel(
 
         def finish(b, terms):
             rows = slice(b * P, (b + 1) * P)
-            total = keep.tile([P, T], F32, name="total%d" % b)
-            queue = nc.scalar if b >= BLOCKS - 3 else nc.sync
+            total = ring.tile([P, T], F32, name="total", bufs=3)
+            queue = nc.scalar if b >= BLOCKS - 4 else nc.sync
             squares = T // P
-            if b == BLOCKS - 2:
-                squares -= ON_VECTOR
+            if b in RELIEVED:
+                squares -= 1
                 cols = slice(squares * P, T)
                 nc.vector.tensor_tensor(total[:, cols], terms[0][:, cols], terms[1][:, cols], ADD)
             third = -(-squares // 3) * P
@@ -240,19 +240,17 @@ def tile_moe_cpy_mlp_silu_kernel(
             pick(b, 1, slice(0, T), terms[1][:])
 
         b = BLOCKS - 1
-        pieces = [slice(0, T // 2), slice(T // 2, 7 * T // 8), slice(7 * T // 8, T)]
-        last = new_terms()
+        pieces = [slice(0, T // 2), slice(T // 2, 3 * T // 4), slice(3 * T // 4, 7 * T // 8), slice(7 * T // 8, T)]
+        last = new_terms() + [keep.tile([P, T], F32, name="last")]
 
         def finish_piece(cols):
             nc.vector.tensor_tensor(last[2][:, cols], last[0][:, cols], last[1][:, cols], ADD)
             nc.sync.dma_start(out[b * P : (b + 1) * P, cols], last[2][:, cols])
 
-        for i, cols in enumerate(pieces):
-            pick(b, 0, cols, last[0][:, cols])
-            if i == 0:
-                finish(b - 1, terms)
-                last.append(ring.tile([P, T], F32, name="last", tag="turned_sum", bufs=2))
-            else:
-                finish_piece(pieces[i - 1])
+        pick(b, 0, slice(0, T), last[0][:])
+        finish(b - 1, terms)
+        pick(b, 1, pieces[0], last[1][:, pieces[0]])
+        for before, cols in zip(pieces, pieces[1:]):
             pick(b, 1, cols, last[1][:, cols])
+            finish_piece(before)
         finish_piece(pieces[-1])

from contextlib import ExitStack

import concourse.mybir as mybir
from concourse.masks import make_identity

K, T, E, C, H, PAD = 1024, 1024, 4, 128, 512, 64
P = 128
SLOTS = E * C
WIN = SLOTS + T + PAD
PASSES = K // 512
BLOCKS = K // P
BANK = 512
RUN = T // P
RELIEVED = range(2, BLOCKS - 1)

F32 = mybir.dt.float32
BF16 = mybir.dt.bfloat16
I32 = mybir.dt.int32
U32 = mybir.dt.uint32
U16 = mybir.dt.uint16
U8 = mybir.dt.uint8
FP8X4 = mybir.dt.float8_e4m3fn_x4
MULT = mybir.AluOpType.mult
ADD = mybir.AluOpType.add
SILU = mybir.ActivationFunctionType.Silu

FLOPS = 2 * 2 * SLOTS * K * H


def tile_moe_cpy_mlp_silu_kernel(
    tc, x_words, x_scales, xr, w1_words, w1_scales, w2_words, w2_scales, gate, offs, pos1, pos2, out
):
    nc = tc.nc
    with ExitStack() as ctx:
        keep = ctx.enter_context(tc.tile_pool(name="keep", bufs=1))
        ring = ctx.enter_context(tc.tile_pool(name="ring", bufs=4))
        psum = ctx.enter_context(tc.psum_pool(name="psum", bufs=2))

        offs_sb = keep.tile([P, SLOTS // 16], U16, name="offs_sb")
        pos_sb = [keep.tile([P, T // 16], U16, name="pos_sb%d" % r) for r in range(2)]
        xw = [keep.tile([P, T], I32, name="xw%d" % s, align_bytes=64) for s in range(PASSES)]
        xs = keep.tile([P, T], U8, name="xs", align_bytes=64)
        w1 = keep.tile([P, E, PASSES, H], I32, name="w1", align_bytes=64)
        w1s = [keep.tile([P, H], U8, name="w1s%d" % r, align_bytes=64) for r in range(2)]
        w2 = keep.tile([P, E, K], I32, name="w2", align_bytes=64)
        w2s = keep.tile([P, K], U8, name="w2s", align_bytes=64)
        gates = [keep.tile([P, T], F32, name="gates%d" % r) for r in range(2)]
        gate_row = keep.tile([P, 2, RUN], F32, name="gate_row")
        window = [keep.tile([P, WIN], F32, name="window%d" % b) for b in range(BLOCKS)]
        ident = keep.tile([P, P], F32, name="ident")

        nc.gpsimd.memset(xs[:].bitcast(I32), 0)
        for r in range(2):
            nc.vector.memset(w1s[r][:].bitcast(I32), 0)
        nc.vector.memset(w2s[:].bitcast(I32), 0)
        for b in range(BLOCKS):
            nc.vector.memset(window[b][:, SLOTS + T :], 0.0)
        make_identity(nc, ident[:])

        w1_hbm = w1_words.rearrange("e s p i d -> p e s (i d)").bitcast(I32)
        w2_hbm = w2_words.rearrange("e s p n d -> p (e s) (n d)").bitcast(I32)

        def load_x(s):
            nc.sync.dma_start(xw[s][:], x_words[s].rearrange("p t d -> p (t d)").bitcast(I32))

        def load_w1(e, passes, cols):
            nc.sync.dma_start(w1[:, e, passes, cols], w1_hbm[:, e, passes, cols])

        def load_w2(first, last):
            cols = slice(first * P, last * P)
            nc.sync.dma_start(w2[:, :, cols], w2_hbm[:, :, cols])

        def load_xr(b):
            nc.sync.dma_start(window[b][:, SLOTS : SLOTS + T], xr[b * P : (b + 1) * P, :])

        halves = [slice(0, T // 2), slice(T // 2, T)]

        def load_w1_scales(r):
            planes = w1_scales.rearrange("e s b i -> (e s) b i")[4 * r : 4 * r + 4]
            for q in range(4):
                nc.sync.dma_start(w1s[r][32 * q : 32 * q + 16, :].bitcast(I32), planes[:, 4 * q : 4 * q + 4, :].bitcast(I32))

        parts = [[slice(0, H)]] * E
        nc.sync.dma_start(offs_sb[:], offs)
        nc.sync.dma_start(gate_row[:], gate[:, 0, :].rearrange("r (p m) -> p r m", m=RUN))
        load_x(0)
        for q in range(4):
            nc.sync.dma_start(
                xs[32 * q : 32 * q + 4 * PASSES, :].bitcast(I32),
                x_scales[:, 4 * q : 4 * q + 4, :].bitcast(I32),
            )
        load_x(1)
        load_w1(0, slice(0, PASSES), slice(0, H))
        load_w1_scales(0)
        load_w1(1, slice(0, PASSES), slice(0, H))
        load_w1(2, slice(0, PASSES), slice(0, H))
        load_w1_scales(1)
        load_w1(E - 1, 0, slice(0, H))
        load_w1(E - 1, 1, slice(0, H))
        load_w2(0, 1)
        for q in range(4):
            nc.sync.dma_start(
                w2s[32 * q : 32 * q + 4 * E, :].bitcast(I32),
                w2_scales[:, 0, 4 * q : 4 * q + 4, :].bitcast(I32),
            )
        load_xr(0)
        for r, pos in enumerate((pos1, pos2)):
            nc.sync.dma_start(pos_sb[r][:], pos)
        load_w2(1, 4)
        load_w2(4, 8)
        load_xr(1)
        for b in range(2, BLOCKS):
            load_xr(b)

        for r in range(2):
            for half in range(2):
                spread = psum.tile([P, RUN // 2, P], F32, name="spread", tag="y", bufs=4)
                for j in range(RUN // 2):
                    col = half * RUN // 2 + j
                    nc.tensor.transpose(spread[:, j, :], gate_row[:, r, col : col + 1].to_broadcast([P, P]), ident[:])
                nc.scalar.copy(
                    gates[r][:].rearrange("q (p h j) -> q h p j", h=2, j=RUN // 2)[:, half, :, :],
                    spread[:].rearrange("q j p -> q p j"),
                )

        xsg = keep.tile([P, SLOTS], U8, name="xsg", align_bytes=64)
        xg = [keep.tile([P, SLOTS], U32, name="xg%d" % s, align_bytes=64) for s in range(PASSES)]
        for slots in (slice(0, SLOTS // 2), slice(SLOTS // 2, SLOTS)):
            part_offs = offs_sb[:, slots.start // 16 : slots.stop // 16]
            nc.vector.tensor_copy(xg[0][:, slots], xw[0][:].bitcast(U32).indirect(part_offs))
            nc.vector.tensor_copy(xsg[:, slots], xs[:].indirect(part_offs))
            nc.vector.tensor_copy(xg[1][:, slots], xw[1][:].bitcast(U32).indirect(part_offs))

        h_codes = [keep.tile([P, C], U32, name="h_codes%d" % e, align_bytes=64) for e in range(E)]
        h_scales = [keep.tile([P, C], U8, name="h_scales%d" % e, align_bytes=64) for e in range(E)]

        def first_layer(e):
            cols = slice(e * C, (e + 1) * C)
            act = ring.tile([P, 2, P, 2], BF16, name="act")
            for part in parts[e]:
                pre = psum.tile([P, part.stop - part.start], F32, name="pre", tag="pre" if part.start == 0 else "summed")
                for s in range(PASSES):
                    nc.tensor.matmul_mx(
                        out=pre[:],
                        lhsT=xg[s][:, cols].bitcast(FP8X4),
                        lhsT_scale=xsg[4 * s :, cols],
                        rhs=w1[:, e, s, part].bitcast(FP8X4),
                        rhs_scale=w1s[e // 2][4 * (PASSES * (e % 2) + s) :, part],
                        start=(s == 0),
                        stop=(s == PASSES - 1),
                    )
                nc.scalar.activation(
                    act[:, :, part.start // 4 : part.stop // 4, :],
                    pre[:].rearrange("c (p u j) -> c u p j", u=2, j=2),
                    SILU,
                )
            pairs = act[:].rearrange("c u p j -> c (u p j)").bitcast(F32)
            turned = psum.tile([P, 2, C], F32, name="turned", tag="back")
            for u in range(2):
                nc.tensor.transpose(turned[:, u, :], pairs[:, u * P : (u + 1) * P], ident[:])
            grouped = ring.tile([P, 4 * C], BF16, name="grouped", align_bytes=64)
            move = nc.scalar.copy if e == E - 1 else nc.vector.tensor_copy
            move(grouped[:].bitcast(F32).rearrange("p (c u) -> p c u", u=2), turned[:].rearrange("p u c -> p c u"))
            nc.vector.quantize_mx(out=h_codes[e][:].bitcast(FP8X4), scales=h_scales[e][:], in_=grouped[:])

        def expert_rows(y, b, e):
            rows = slice(b * P, (b + 1) * P)
            nc.tensor.matmul_mx(
                out=y[:, e * C : (e + 1) * C],
                lhsT=w2[:, e, rows].bitcast(FP8X4),
                lhsT_scale=w2s[4 * e :, rows],
                rhs=h_codes[e][:].bitcast(FP8X4),
                rhs_scale=h_scales[e][:],
                start=True,
                stop=True,
            )

        def second_layer(b):
            y = psum.tile([P, SLOTS], F32, name="y", tag="y", bufs=4)
            for e in range(E):
                expert_rows(y, b, e)
            nc.scalar.copy(window[b][:, :SLOTS], y[:])

        for e in range(E):
            first_layer(e)
        y_early = psum.tile([P, (E - 1) * C], F32, name="y_early", tag="y", bufs=4)
        for e in range(E - 1):
            expert_rows(y_early, 0, e)
        nc.vector.tensor_copy(window[0][:, : (E - 1) * C], y_early[:])
        y_late = psum.tile([P, SLOTS], F32, name="y_late", tag="y", bufs=4)
        expert_rows(y_late, 0, E - 1)
        nc.scalar.copy(window[0][:, (E - 1) * C : SLOTS], y_late[:, (E - 1) * C :])

        def pick(b, r, cols, dst):
            lists = pos_sb[r][:, cols.start // 16 : cols.stop // 16]
            nc.vector.tensor_tensor(dst, window[b][:].indirect(lists), gates[r][:, cols], MULT)

        def new_terms():
            return [ring.tile([P, T], F32, name="term%d" % r, bufs=3) for r in range(2)]

        def finish(b, terms):
            rows = slice(b * P, (b + 1) * P)
            total = ring.tile([P, T], F32, name="total", bufs=3)
            queue = nc.scalar if b >= BLOCKS - 4 else nc.sync
            squares = T // P
            if b in RELIEVED:
                squares -= 1
                cols = slice(squares * P, T)
                nc.vector.tensor_tensor(total[:, cols], terms[0][:, cols], terms[1][:, cols], ADD)
            third = -(-squares // 3) * P
            turned_sum = ring.tile([P, T], F32, name="turned_sum", bufs=2)
            for first in range(0, squares * P, third):
                cols = slice(first, min(first + third, squares * P))
                summed = psum.tile([P, cols.stop - cols.start], F32, name="summed", tag="y", bufs=4)
                for j in range(cols.start, cols.stop, P):
                    for r in range(2):
                        nc.tensor.matmul(
                            summed[:, j - cols.start : j - cols.start + P], terms[r][:, j : j + P], ident[:],
                            start=(r == 0), stop=(r == 1), is_transpose=True,
                        )
                nc.scalar.copy(turned_sum[:, cols], summed[:])
            for first in range(0, squares * P, BANK):
                cols = slice(first, min(first + BANK, squares * P))
                back = psum.tile([P, cols.stop - cols.start], F32, name="back", tag="y", bufs=4)
                for j in range(cols.start, cols.stop, P):
                    nc.tensor.transpose(back[:, j - cols.start : j - cols.start + P], turned_sum[:, j : j + P], ident[:])
                nc.scalar.copy(total[:, cols], back[:])
                queue.dma_start(out[rows, first : first + BANK], total[:, first : first + BANK])

        for b in range(1, BLOCKS):
            second_layer(b)
        terms = new_terms()
        for r in range(2):
            pick(0, r, slice(0, T), terms[r][:])
        for b in range(1, BLOCKS - 1):
            before = terms
            terms = new_terms()
            pick(b, 0, slice(0, T), terms[0][:])
            finish(b - 1, before)
            pick(b, 1, slice(0, T), terms[1][:])

        b = BLOCKS - 1
        pieces = [slice(0, T // 2), slice(T // 2, 3 * T // 4), slice(3 * T // 4, 7 * T // 8), slice(7 * T // 8, T)]
        last = new_terms() + [keep.tile([P, T], F32, name="last")]

        def finish_piece(cols):
            nc.vector.tensor_tensor(last[2][:, cols], last[0][:, cols], last[1][:, cols], ADD)
            nc.sync.dma_start(out[b * P : (b + 1) * P, cols], last[2][:, cols])

        pick(b, 0, slice(0, T), last[0][:])
        finish(b - 1, terms)
        pick(b, 1, pieces[0], last[1][:, pieces[0]])
        for before, cols in zip(pieces, pieces[1:]):
            pick(b, 1, cols, last[1][:, cols])
            finish_piece(before)
        finish_piece(pieces[-1])
